import numpy as np
import ml_dtypes


def mxq(x, axis, fmt="e4m3"):
    dtype, down = {"e4m3": (ml_dtypes.float8_e4m3fn, 7), "e5m2": (ml_dtypes.float8_e5m2, 14)}[fmt]
    v = np.moveaxis(np.asarray(x, np.float32).astype(ml_dtypes.bfloat16).astype(np.float64), axis, -1)
    blocks = v.reshape(v.shape[:-1] + (-1, 32))
    amax = np.abs(blocks).max(-1, keepdims=True)
    byte = np.maximum(np.where(amax > 0, np.frexp(amax)[1] - 1 + 127, 0) - down, 1)
    scale = np.exp2(byte - 127.0)
    codes = (blocks / scale).astype(np.float32).astype(dtype).astype(np.float64)
    return np.moveaxis((codes * scale).reshape(v.shape), -1, axis)


WIDE = False


def mx_kscale(k):
    if not WIDE:
        return np.ones(k)
    levels = np.array([10, -10, 5, -5, 0])
    if k % 512:
        return np.exp2(np.random.permutation(np.resize(levels, k // 32))).repeat(32)
    a = np.empty((k // 512, 16))
    for p in range(k // 512):
        a[p, :8] = np.random.permutation(np.resize(levels, 8))
        for g in range(8):
            far = levels[np.abs(levels - a[p, g]) >= 10]
            a[p, g + 8] = far[np.random.randint(len(far))]
    return np.exp2(a.ravel()).repeat(32)


def f64(x):
    return np.asarray(x).astype(np.float64)


def striped(idx):
    return np.tile(idx.reshape(-1, 16).T, (8, 1)).astype(np.uint16)


def unstriped(offs):
    return offs[:16].T.reshape(-1).astype(np.int64)


E2M1 = np.array([0.0, 0.5, 1.0, 1.5, 2.0, 3.0, 4.0, 6.0, -0.0, -0.5, -1.0, -1.5, -2.0, -3.0, -4.0, -6.0])


def pack_weight(w, fmt):
    k, n = w.shape
    w = f64(np.asarray(w, np.float32).astype(ml_dtypes.bfloat16)).reshape(k // 32, 32, n)
    amax = np.abs(w).max(1)
    if fmt == "e4m3":
        byte = np.frexp(amax)[1] - 1 + 127 - 7
    else:
        mant, ex = np.frexp(amax / 6.0)
        byte = np.where(mant > 0.5, ex, ex - 1) + 127
    byte = np.clip(np.where(amax > 0, byte, 1), 1, 254)
    scaled = (w * np.exp2(127.0 - byte)[:, None, :]).reshape(k, n).astype(np.float32)
    by_word = np.ascontiguousarray(scaled.reshape(k // 512, 128, 4, n).transpose(0, 1, 3, 2))
    if fmt == "e4m3":
        words = by_word.astype(ml_dtypes.float8_e4m3fn).view(np.uint8)
    else:
        c = by_word.astype(ml_dtypes.float4_e2m1fn).view(np.uint8) & 0xF
        words = (c[..., 0::2] | (c[..., 1::2] << 4)).reshape(k // 512, 128, 2 * n)
    return np.ascontiguousarray(words), np.ascontiguousarray(byte.astype(np.uint8).reshape(k // 512, 16, n))


def unpack_weight(words, scales, fmt):
    g, _, n = scales.shape
    words = np.ascontiguousarray(words).reshape(g, 128, n, -1)
    if fmt == "e4m3":
        vals = words.view(ml_dtypes.float8_e4m3fn).astype(np.float64)
    else:
        nib = np.empty((g, 128, n, 4), np.uint8)
        nib[..., 0::2] = words & 0xF
        nib[..., 1::2] = words >> 4
        vals = E2M1[nib]
    vals = vals * np.repeat(np.exp2(scales.astype(np.float64) - 127.0), 8, axis=1)[..., None]
    return vals.transpose(0, 1, 3, 2).reshape(g * 512, n)


def gelu(v):
    return 0.5 * v * (1.0 + np.tanh(np.sqrt(2.0 / np.pi) * (v + 0.044715 * v**3)))


def striped8(idx):
    return np.concatenate([v.reshape(-1, 16).T for v in idx]).astype(np.uint16)


def unstriped8(offs):
    return np.stack([offs[16 * g:16 * g + 16].T.reshape(-1) for g in range(8)]).astype(np.int64)


def heads(h, wgt, idx8):
    r = np.arange(h.shape[0])
    return wgt[r // 4 % 128] * h[r[:, None], idx8[r % 512 // 64]]


def put_heads(h, wgs, idx8, t2):
    r = np.arange(h.shape[0])
    page = np.zeros((h.shape[0], t2))
    page[r[:, None], idx8[r % 512 // 64]] = wgs[r // 4 % 128] * h
    return page


T, S, P, T2, K, H, M, N = 2048, 512, 512, 1024, 1536, 1024, 512, 256

def setup_inputs():
    n = np.random.standard_normal
    s = mx_kscale(K)[:, None]
    u = mx_kscale(H)[:, None]
    u2 = mx_kscale(M)[:, None]
    d = {}
    d["tab_words"], d["tab_scales"] = pack_weight(n((K, T)) * s, "e4m3")
    d["offs"] = striped(np.random.permutation(T)[:S])
    d["offs2"] = striped8(np.stack([np.random.permutation(T2)[:S] for _ in range(8)]))
    d["offs3"] = striped8(np.stack([np.random.permutation(T2)[:P] for _ in range(8)]))
    d["w1"] = (n((K, H)) / K ** 0.5 / s).astype(np.float32)
    d["gain1"] = (np.exp(0.4 * n(H)) * u[:, 0]).astype(np.float32)
    d["wgs"] = np.repeat(np.random.uniform(0.5, 2.0, (8, S)), 16, axis=0).astype(np.float32)
    d["wgt"] = np.repeat(np.random.uniform(0.5, 2.0, (8, P)), 16, axis=0).astype(np.float32)
    d["ink"] = (n((H, P)) * u).astype(np.float32)
    d["w2_words"], d["w2_scales"] = pack_weight(n((H, M)) / H ** 0.5 / u, "e2m1")
    d["b2"] = (0.6 * n(M)).astype(np.float32)
    d["gain2"] = (np.exp(0.4 * n(M)) * u2[:, 0]).astype(np.float32)
    d["w3"] = (n((M, N)) / M ** 0.5 / u2).astype(np.float32)
    return d

def reference(tab_words, tab_scales, offs, offs2, offs3, w1, gain1, wgs, wgt, ink,
              w2_words, w2_scales, b2, gain2, w3):
    v = unpack_weight(tab_words, tab_scales, "e4m3")[:, unstriped(offs)]
    h = f64(gain1)[:, None] * (mxq(f64(w1), 0, "e4m3").T @ v)
    page = put_heads(h, f64(wgs), unstriped8(offs2), T2)
    x = heads(page, f64(wgt), unstriped8(offs3))
    z = mxq(x + f64(ink), 0, "e4m3")
    w2 = unpack_weight(w2_words, w2_scales, "e2m1")
    y = np.tanh((w2.T @ z) + f64(b2)[:, None])
    yq = mxq(f64(gain2)[:, None] * y, 0, "e4m3")
    return mxq(f64(w3), 0, "e4m3").T @ yq

@@ -1,0 +1,277 @@
+from contextlib import ExitStack
+
+import concourse.mybir as mybir
+from concourse.masks import make_identity
+
+T, S, T2, K, H, M, N = 2048, 512, 1024, 1536, 1024, 512, 256
+FLOPS = 2 * S * (K * H + H * M + M * N)
+
+F32 = mybir.dt.float32
+BF16 = mybir.dt.bfloat16
+I32 = mybir.dt.int32
+U32 = mybir.dt.uint32
+U16 = mybir.dt.uint16
+U8 = mybir.dt.uint8
+FP8X4 = mybir.dt.float8_e4m3fn_x4
+FP4X4 = mybir.dt.float4_e2m1fn_x4
+MULT = mybir.AluOpType.mult
+ADD = mybir.AluOpType.add
+COPY = mybir.ActivationFunctionType.Copy
+TANH = mybir.ActivationFunctionType.Tanh
+
+P = 128
+PACK = 4
+KP = P * PACK
+PASSES1 = K // KP
+HALVES = H // KP
+CH = 128
+CHUNKS = S // CH
+
+
+def tile_list_scanner_recount_features_kernel(
+    tc, tab_words, tab_scales, offs, offs2, offs3, w1, gain1, wgs, wgt, ink,
+    w2_words, w2_scales, b2, gain2, w3, out,
+):
+    nc = tc.nc
+    with ExitStack() as ctx:
+        lists = ctx.enter_context(tc.tile_pool(name="lists", bufs=1))
+        keep = ctx.enter_context(tc.tile_pool(name="keep", bufs=1))
+        psum = ctx.enter_context(tc.psum_pool(name="psum", bufs=1))
+
+        def sb(shape, dtype, name, tag=None):
+            return keep.tile(shape, dtype, name=name, tag=tag or name, align_bytes=64)
+
+        def bank(shape, name, tag):
+            return psum.tile(shape, F32, name=name, tag=tag)
+
+        def quantize(grouped, name):
+            width = grouped.shape[1] // PACK
+            codes = sb([P, width], U32, name + "_codes")
+            scales = sb([P, width], U8, name + "_scales")
+            nc.vector.quantize_mx(out=codes[:].bitcast(FP8X4), scales=scales[:], in_=grouped)
+            return codes, scales
+
+        pick = lists.tile([P, S // 16], U16, name="pick")
+        put = lists.tile([P, S // 16], U16, name="put")
+        take = lists.tile([P, S // 16], U16, name="take")
+
+        tab_plane = sb([P, T], U8, "tab_plane")
+        nc.vector.memset(tab_plane[:].bitcast(I32), 0)
+        for q in range(4):
+            nc.scalar.dma_start(
+                out=tab_plane[32 * q : 32 * q + 4 * PASSES1, :].bitcast(I32),
+                in_=tab_scales[:, 4 * q : 4 * q + 4, :].bitcast(I32),
+            )
+        gain1_sb = sb([P, HALVES, PACK], F32, "gain1_sb")
+        pages = [sb([P, T2], F32, "page%d" % t) for t in range(PACK)]
+        for t in range(PACK):
+            nc.vector.memset(pages[t][:], 0.0)
+        w2_plane_raw = sb([P, HALVES, M], U8, "w2_plane_raw")
+        nc.gpsimd.memset(w2_plane_raw[:].rearrange("p b m -> p (b m)").bitcast(I32), 0)
+        vec_rows = sb([P, P], F32, "vec_rows")
+        nc.gpsimd.memset(vec_rows[:], 0.0)
+        ident = sb([P, P], F32, "ident")
+        make_identity(nc, ident[:])
+
+        def load_w1(b, a):
+            raw = sb([P, PACK, KP], F32, "w1_raw_%d_%d" % (b, a), tag="w1_raw%d" % a)
+            rows = w1[a * KP : (a + 1) * KP, b * KP : (b + 1) * KP]
+            nc.sync.dma_start(out=raw[:], in_=rows.rearrange("(p j) c -> p j c", j=PACK))
+            return raw
+
+        def load_tab(a):
+            words = sb([P, T], I32, "tab%d" % a)
+            nc.sync.dma_start(out=words[:], in_=tab_words[a].rearrange("p n i -> p (n i)").bitcast(I32))
+            return words
+
+        def group_w1(raw, b, a):
+            grouped = sb([P, KP * PACK], BF16, "w1_grouped_%d_%d" % (b, a), tag="grouped_%d_%d" % (b, a))
+            nc.scalar.copy(
+                out=grouped[:].rearrange("p (t m j) -> p m j t", t=PACK, j=PACK),
+                in_=raw[:].rearrange("p j (m t) -> p m j t", t=PACK),
+            )
+            return grouped
+
+        raw0 = [None] * PASSES1
+        tabs = [None] * PASSES1
+        raw0[0] = load_w1(0, 0)
+        nc.sync.dma_start(pick[:], offs)
+        raw0[1] = load_w1(0, 1)
+        tabs[0] = load_tab(0)
+        raw0[2] = load_w1(0, 2)
+        tabs[1] = load_tab(1)
+        nc.sync.dma_start(put[:], offs2)
+        nc.sync.dma_start(out=gain1_sb[:], in_=gain1.rearrange("(b p t) -> p b t", b=HALVES, t=PACK))
+        tabs[2] = load_tab(2)
+        wgs_sb = sb([P, S], F32, "wgs_sb")
+        nc.sync.dma_start(out=wgs_sb[:], in_=wgs)
+
+        w1q = {}
+        picked = []
+        picked_plane = sb([P, S], U8, "picked_plane")
+        for a in range(PASSES1):
+            w1q[0, a] = quantize(group_w1(raw0[a], 0, a)[:], "w1_0_%d" % a)
+            got = sb([P, S], U32, "picked%d" % a)
+            nc.vector.tensor_copy(out=got[:], in_=tabs[a][:].bitcast(U32).indirect(pick[:]))
+            picked.append(got)
+            if a == 0:
+                nc.vector.tensor_copy(out=picked_plane[:], in_=tab_plane[:].indirect(pick[:]))
+
+        def first_product(b):
+            acc = [bank([P, S], "h_%d_%d" % (b, t), "wide%d" % t) for t in range(PACK)]
+            for a in range(PASSES1):
+                codes, scales = w1q[b, a]
+                for t in range(PACK):
+                    cols = slice(t * P, (t + 1) * P)
+                    nc.tensor.matmul_mx(
+                        out=acc[t][:],
+                        lhsT=codes[:, cols].bitcast(FP8X4),
+                        lhsT_scale=scales[:, cols],
+                        rhs=picked[a][:].bitcast(FP8X4),
+                        rhs_scale=picked_plane[4 * a : P, :],
+                        start=(a == 0),
+                        stop=(a == PASSES1 - 1),
+                    )
+            for t in range(PACK):
+                h = sb([P, S], F32, "h_sb_%d_%d" % (b, t))
+                nc.scalar.activation(out=h[:], in_=acc[t][:], func=COPY, scale=gain1_sb[:, b, t : t + 1])
+                nc.vector.tensor_tensor(out=pages[t][:].indirect(put[:]), in0=h[:], in1=wgs_sb[:], op=MULT)
+
+        first_product(0)
+
+        raw1 = [load_w1(1, a) for a in range(PASSES1)]
+        nc.sync.dma_start(take[:], offs3)
+        wgt_sb = sb([P, S], F32, "wgt_sb")
+        nc.sync.dma_start(out=wgt_sb[:], in_=wgt)
+        inks = []
+        for b in range(HALVES):
+            ink_sb = sb([P, PACK, S], F32, "ink%d" % b)
+            nc.sync.dma_start(out=ink_sb[:], in_=ink[b * KP : (b + 1) * KP, :].rearrange("(p t) j -> p t j", t=PACK))
+            inks.append(ink_sb)
+        w2_raw = sb([P, HALVES, 2 * M // 4], I32, "w2_raw")
+        nc.sync.dma_start(out=w2_raw[:], in_=w2_words.rearrange("b p c -> p b c").bitcast(I32))
+        for q in range(4):
+            nc.sync.dma_start(
+                out=w2_plane_raw[32 * q : 32 * q + 4, :, :].bitcast(I32),
+                in_=w2_scales[:, 4 * q : 4 * q + 4, :].rearrange("b r m -> r b m").bitcast(I32),
+            )
+        w3_raw = sb([P, PACK, N], F32, "w3_raw")
+        w3_dealt = w3.rearrange("(a t e) n -> t a e n", t=PACK, e=8)
+        for t in range(PACK):
+            nc.sync.dma_start(out=w3_raw[:, t, :], in_=w3_dealt[t])
+        nc.sync.dma_start(
+            out=vec_rows[0:PACK, :].rearrange("t (a e) -> t a e", e=8),
+            in_=b2.rearrange("(a t e) -> t a e", t=PACK, e=8),
+        )
+        nc.sync.dma_start(
+            out=vec_rows[PACK : 2 * PACK, :].rearrange("t (a e) -> t a e", e=8),
+            in_=gain2.rearrange("(a t e) -> t a e", t=PACK, e=8),
+        )
+
+        for a in range(PASSES1):
+            w1q[1, a] = quantize(group_w1(raw1[a], 1, a)[:], "w1_1_%d" % a)
+
+        x0 = sb([P, PACK, S], F32, "x0", tag="grouped_1_2")
+        for t in range(PACK):
+            nc.vector.tensor_tensor(out=x0[:, t, :], in0=pages[t][:].indirect(take[:]), in1=wgt_sb[:], op=MULT)
+
+        first_product(1)
+
+        z0_words = sb([P, S, 2], F32, "z0_words")
+        for c in range(CHUNKS):
+            cols = slice(c * CH, (c + 1) * CH)
+            summed = bank([P, PACK, P], "summed%d" % c, "turn%d" % (c % 2))
+            for t in range(PACK):
+                nc.tensor.matmul(out=summed[:, t, :], lhsT=inks[0][:, t, cols], rhs=ident[:],
+                                 is_transpose=True, start=True, stop=False)
+                nc.tensor.matmul(out=summed[:, t, :], lhsT=x0[:, t, cols], rhs=ident[:],
+                                 is_transpose=True, start=False, stop=True)
+            turned = sb([P, 2, P, 2], BF16, "turned%d" % c, tag="turned%d" % (c % 2))
+            nc.scalar.copy(out=turned[:], in_=summed[:].rearrange("j (u e) p -> j u p e", e=2))
+            turned_words = turned[:].rearrange("j u p e -> j (u p e)").bitcast(F32)
+            back = bank([P, 2, P], "back%d" % c, "back%d" % (c % 2))
+            for u in range(2):
+                nc.tensor.transpose(back[:, u, :], turned_words[:, u * P : (u + 1) * P], ident[:])
+            nc.scalar.copy(out=z0_words[:, cols, :], in_=back[:].rearrange("p u j -> p j u"))
+        z0_codes, z0_scales = quantize(z0_words[:].rearrange("p j u -> p (j u)").bitcast(BF16), "z0")
+
+        w2_codes = sb([P, HALVES, 2 * M], U8, "w2_codes")
+        nc.vector.tensor_copy(
+            out=w2_codes[:].bitcast(I32).rearrange("p b (t a v) -> p b t a v", t=PACK, v=4),
+            in_=w2_raw[:].rearrange("p b (a t v) -> p b t a v", t=PACK, v=4),
+        )
+        w2_plane = sb([P, HALVES, M], U8, "w2_plane")
+        nc.vector.tensor_copy(
+            out=w2_plane[:].bitcast(I32).rearrange("p b (t a v) -> p b t a v", t=PACK, v=2),
+            in_=w2_plane_raw[:].bitcast(I32).rearrange("p b (a t v) -> p b t a v", t=PACK, v=2),
+        )
+        vec_turned = bank([P, P], "vec_turned", "back0")
+        nc.tensor.transpose(vec_turned[:], vec_rows[:], ident[:])
+        vec = sb([P, 2 * PACK], F32, "vec")
+        nc.scalar.copy(out=vec[:], in_=vec_turned[:, 0 : 2 * PACK])
+        w3_grouped = sb([P, N * PACK], BF16, "w3_grouped")
+        nc.scalar.copy(
+            out=w3_grouped[:].rearrange("p (c i t) -> p c t i", i=4, t=PACK),
+            in_=w3_raw[:].rearrange("p t (c i) -> p c t i", i=4),
+        )
+
+        x1 = sb([P, PACK, S], F32, "x1")
+        for t in range(PACK - 1):
+            nc.vector.tensor_tensor(out=x1[:, t, :], in0=pages[t][:].indirect(take[:]), in1=wgt_sb[:], op=MULT)
+        acc2 = [bank([P, S], "y_%d" % t, "wide%d" % t) for t in range(PACK)]
+        ys = []
+        for c in range(CHUNKS):
+            cols = slice(c * CH, (c + 1) * CH)
+            entries = take[:, c * CH // 16 : (c + 1) * CH // 16]
+            t = PACK - 1
+            nc.vector.tensor_tensor(out=x1[:, t, cols], in0=pages[t][:].indirect(entries), in1=wgt_sb[:, cols], op=MULT)
+            z1 = sb([P, CH * PACK], BF16, "z1_%d" % c)
+            nc.vector.tensor_tensor(
+                out=z1[:].rearrange("p (c i t) -> p c t i", i=4, t=PACK),
+                in0=x1[:, :, cols].rearrange("p t (c i) -> p c t i", i=4),
+                in1=inks[1][:, :, cols].rearrange("p t (c i) -> p c t i", i=4),
+                op=ADD,
+            )
+            z1_codes, z1_scales = quantize(z1[:], "z1_%d" % c)
+            y = sb([P, PACK, CH], F32, "y_sb%d" % c)
+            for t in range(PACK):
+                for b, codes, scales in ((0, z0_codes[:, cols], z0_scales[:, cols]), (1, z1_codes[:], z1_scales[:])):
+                    nc.tensor.matmul_mx(
+                        out=acc2[t][:, cols],
+                        lhsT=w2_codes[:, b, 2 * t * P : 2 * (t + 1) * P].bitcast(FP4X4),
+                        lhsT_scale=w2_plane[:, b, t * P : (t + 1) * P],
+                        rhs=codes.bitcast(FP8X4),
+                        rhs_scale=scales,
+                        start=(b == 0),
+                        stop=(b == 1),
+                    )
+                nc.scalar.activation(out=y[:, t, :], in_=acc2[t][:, cols], func=TANH, bias=vec[:, t : t + 1])
+            ys.append(y)
+
+        w3_codes, w3_scales = quantize(w3_grouped[:], "w3")
+        gain2_wide = vec[:, PACK : 2 * PACK].unsqueeze(1).unsqueeze(3).to_broadcast([P, CH // 4, PACK, 4])
+        out_rows = out.rearrange("(n p) j -> p n j", p=P)
+        for c in range(CHUNKS):
+            cols = slice(c * CH, (c + 1) * CH)
+            y_grouped = sb([P, CH * PACK], BF16, "y_grouped%d" % c)
+            nc.vector.tensor_tensor(
+                out=y_grouped[:].rearrange("p (c i t) -> p c t i", i=4, t=PACK),
+                in0=ys[c][:].rearrange("p t (c i) -> p c t i", i=4),
+                in1=gain2_wide,
+                op=MULT,
+            )
+            y_codes, y_scales = quantize(y_grouped[:], "y%d" % c)
+            acc3 = bank([P, N // P, CH], "acc3_%d" % c, "turn%d" % (c % 2))
+            for n in range(N // P):
+                nc.tensor.matmul_mx(
+                    out=acc3[:, n, :],
+                    lhsT=w3_codes[:, n * P : (n + 1) * P].bitcast(FP8X4),
+                    lhsT_scale=w3_scales[:, n * P : (n + 1) * P],
+                    rhs=y_codes[:].bitcast(FP8X4),
+                    rhs_scale=y_scales[:],
+                    start=True,
+                    stop=True,
+                )
+            result = sb([P, N // P, CH], F32, "result%d" % c)
+            nc.scalar.copy(out=result[:], in_=acc3[:])
+            nc.sync.dma_start(out=out_rows[:, :, cols], in_=result[:])

@@ -57,26 +57,25 @@ def tile_list_scanner_recount_features_kernel(
 
         tab_plane = sb([P, T], U8, "tab_plane")
         nc.vector.memset(tab_plane[:].bitcast(I32), 0)
-        for q in range(4):
-            nc.scalar.dma_start(
-                out=tab_plane[32 * q : 32 * q + 4 * PASSES1, :].bitcast(I32),
-                in_=tab_scales[:, 4 * q : 4 * q + 4, :].bitcast(I32),
-            )
         gain1_sb = sb([P, HALVES, PACK], F32, "gain1_sb")
+        vec_rows = sb([P, P], F32, "vec_rows")
+        nc.vector.memset(vec_rows[:], 0.0)
+        warm = sb([P, 1], F32, "warm")
+        nc.scalar.activation(out=warm[:], in_=vec_rows[:, 0:1], func=TANH)
         pages = [sb([P, T2], F32, "page%d" % t) for t in range(PACK)]
         for t in range(PACK):
             nc.vector.memset(pages[t][:], 0.0)
         w2_plane_raw = sb([P, HALVES, M], U8, "w2_plane_raw")
         nc.gpsimd.memset(w2_plane_raw[:].rearrange("p b m -> p (b m)").bitcast(I32), 0)
-        vec_rows = sb([P, P], F32, "vec_rows")
-        nc.gpsimd.memset(vec_rows[:], 0.0)
         ident = sb([P, P], F32, "ident")
         make_identity(nc, ident[:])
 
-        def load_w1(b, a):
+        def load_w1(b, a, pieces=1):
             raw = sb([P, PACK, KP], F32, "w1_raw_%d_%d" % (b, a), tag="w1_raw%d" % a)
-            rows = w1[a * KP : (a + 1) * KP, b * KP : (b + 1) * KP]
-            nc.sync.dma_start(out=raw[:], in_=rows.rearrange("(p j) c -> p j c", j=PACK))
+            rows = w1[a * KP : (a + 1) * KP, b * KP : (b + 1) * KP].rearrange("(p j) c -> p j c", j=PACK)
+            step = PACK // pieces
+            for j in range(0, PACK, step):
+                nc.sync.dma_start(out=raw[:, j : j + step, :], in_=rows[:, j : j + step, :])
             return raw
 
         def load_tab(a):
@@ -94,14 +93,19 @@ def tile_list_scanner_recount_features_kernel(
 
         raw0 = [None] * PASSES1
         tabs = [None] * PASSES1
-        raw0[0] = load_w1(0, 0)
+        raw0[0] = load_w1(0, 0, 2)
+        raw0[1] = load_w1(0, 1, 2)
         nc.sync.dma_start(pick[:], offs)
-        raw0[1] = load_w1(0, 1)
-        tabs[0] = load_tab(0)
-        raw0[2] = load_w1(0, 2)
-        tabs[1] = load_tab(1)
         nc.sync.dma_start(put[:], offs2)
         nc.sync.dma_start(out=gain1_sb[:], in_=gain1.rearrange("(b p t) -> p b t", b=HALVES, t=PACK))
+        tabs[0] = load_tab(0)
+        for q in range(4):
+            nc.sync.dma_start(
+                out=tab_plane[32 * q : 32 * q + 4 * PASSES1, :].bitcast(I32),
+                in_=tab_scales[:, 4 * q : 4 * q + 4, :].bitcast(I32),
+            )
+        raw0[2] = load_w1(0, 2)
+        tabs[1] = load_tab(1)
         tabs[2] = load_tab(2)
         wgs_sb = sb([P, S], F32, "wgs_sb")
         nc.sync.dma_start(out=wgs_sb[:], in_=wgs)
@@ -112,30 +116,42 @@ def tile_list_scanner_recount_features_kernel(
         for a in range(PASSES1):
             w1q[0, a] = quantize(group_w1(raw0[a], 0, a)[:], "w1_0_%d" % a)
             got = sb([P, S], U32, "picked%d" % a)
-            nc.vector.tensor_copy(out=got[:], in_=tabs[a][:].bitcast(U32).indirect(pick[:]))
+            pieces = 2 if a == PASSES1 - 1 else 1
+            for s in range(pieces):
+                w = S // pieces
+                nc.vector.tensor_copy(
+                    out=got[:, s * w : (s + 1) * w],
+                    in_=tabs[a][:].bitcast(U32).indirect(pick[:, s * w // 16 : (s + 1) * w // 16]),
+                )
             picked.append(got)
             if a == 0:
                 nc.vector.tensor_copy(out=picked_plane[:], in_=tab_plane[:].indirect(pick[:]))
 
         def first_product(b):
-            acc = [bank([P, S], "h_%d_%d" % (b, t), "wide%d" % t) for t in range(PACK)]
+            units = [(t, 0, S, "wide%d" % t) for t in range(PACK)]
+            if b == 0:
+                units = [(0, 0, S // 2, "turn0"), (0, S // 2, S // 2, "wide0")] + units[1:]
+            acc = [bank([P, w], "h_%d_%d_%d" % (b, t, j0), tag) for t, j0, w, tag in units]
             for a in range(PASSES1):
                 codes, scales = w1q[b, a]
-                for t in range(PACK):
+                for (t, j0, w, tag), ps in zip(units, acc):
                     cols = slice(t * P, (t + 1) * P)
                     nc.tensor.matmul_mx(
-                        out=acc[t][:],
+                        out=ps[:],
                         lhsT=codes[:, cols].bitcast(FP8X4),
                         lhsT_scale=scales[:, cols],
-                        rhs=picked[a][:].bitcast(FP8X4),
-                        rhs_scale=picked_plane[4 * a : P, :],
+                        rhs=picked[a][:, j0 : j0 + w].bitcast(FP8X4),
+                        rhs_scale=picked_plane[4 * a : P, j0 : j0 + w],
                         start=(a == 0),
                         stop=(a == PASSES1 - 1),
                     )
-            for t in range(PACK):
-                h = sb([P, S], F32, "h_sb_%d_%d" % (b, t))
-                nc.scalar.activation(out=h[:], in_=acc[t][:], func=COPY, scale=gain1_sb[:, b, t : t + 1])
-                nc.vector.tensor_tensor(out=pages[t][:].indirect(put[:]), in0=h[:], in1=wgs_sb[:], op=MULT)
+            for (t, j0, w, tag), ps in zip(units, acc):
+                h = sb([P, w], F32, "h_sb_%d_%d_%d" % (b, t, j0))
+                nc.scalar.activation(out=h[:], in_=ps[:], func=COPY, scale=gain1_sb[:, b, t : t + 1])
+                nc.vector.tensor_tensor(
+                    out=pages[t][:].indirect(put[:, j0 // 16 : (j0 + w) // 16]),
+                    in0=h[:], in1=wgs_sb[:, j0 : j0 + w], op=MULT,
+                )
 
         first_product(0)
 
@@ -219,21 +235,30 @@ def tile_list_scanner_recount_features_kernel(
         for t in range(PACK - 1):
             nc.vector.tensor_tensor(out=x1[:, t, :], in0=pages[t][:].indirect(take[:]), in1=wgt_sb[:], op=MULT)
         acc2 = [bank([P, S], "y_%d" % t, "wide%d" % t) for t in range(PACK)]
-        ys = []
-        for c in range(CHUNKS):
+        gain2_wide = vec[:, PACK : 2 * PACK].unsqueeze(1).unsqueeze(3).to_broadcast([P, CH // 4, PACK, 4])
+        out_rows = out.rearrange("(n p) j -> p n j", p=P)
+        z1, ys, y_grouped = {}, {}, {}
+
+        def read_last(c):
             cols = slice(c * CH, (c + 1) * CH)
             entries = take[:, c * CH // 16 : (c + 1) * CH // 16]
             t = PACK - 1
             nc.vector.tensor_tensor(out=x1[:, t, cols], in0=pages[t][:].indirect(entries), in1=wgt_sb[:, cols], op=MULT)
-            z1 = sb([P, CH * PACK], BF16, "z1_%d" % c)
+
+        def add_ink(c):
+            cols = slice(c * CH, (c + 1) * CH)
+            z1[c] = sb([P, CH * PACK], BF16, "z1_%d" % c)
             nc.vector.tensor_tensor(
-                out=z1[:].rearrange("p (c i t) -> p c t i", i=4, t=PACK),
+                out=z1[c][:].rearrange("p (c i t) -> p c t i", i=4, t=PACK),
                 in0=x1[:, :, cols].rearrange("p t (c i) -> p c t i", i=4),
                 in1=inks[1][:, :, cols].rearrange("p t (c i) -> p c t i", i=4),
                 op=ADD,
             )
-            z1_codes, z1_scales = quantize(z1[:], "z1_%d" % c)
-            y = sb([P, PACK, CH], F32, "y_sb%d" % c)
+
+        def second_product(c):
+            cols = slice(c * CH, (c + 1) * CH)
+            z1_codes, z1_scales = quantize(z1[c][:], "z1_%d" % c)
+            ys[c] = sb([P, PACK, CH], F32, "y_sb%d" % c)
             for t in range(PACK):
                 for b, codes, scales in ((0, z0_codes[:, cols], z0_scales[:, cols]), (1, z1_codes[:], z1_scales[:])):
                     nc.tensor.matmul_mx(
@@ -245,22 +270,20 @@ def tile_list_scanner_recount_features_kernel(
                         start=(b == 0),
                         stop=(b == 1),
                     )
-                nc.scalar.activation(out=y[:, t, :], in_=acc2[t][:, cols], func=TANH, bias=vec[:, t : t + 1])
-            ys.append(y)
+                nc.scalar.activation(out=ys[c][:, t, :], in_=acc2[t][:, cols], func=TANH, bias=vec[:, t : t + 1])
 
-        w3_codes, w3_scales = quantize(w3_grouped[:], "w3")
-        gain2_wide = vec[:, PACK : 2 * PACK].unsqueeze(1).unsqueeze(3).to_broadcast([P, CH // 4, PACK, 4])
-        out_rows = out.rearrange("(n p) j -> p n j", p=P)
-        for c in range(CHUNKS):
-            cols = slice(c * CH, (c + 1) * CH)
-            y_grouped = sb([P, CH * PACK], BF16, "y_grouped%d" % c)
+        def apply_gain2(c):
+            y_grouped[c] = sb([P, CH * PACK], BF16, "y_grouped%d" % c)
             nc.vector.tensor_tensor(
-                out=y_grouped[:].rearrange("p (c i t) -> p c t i", i=4, t=PACK),
+                out=y_grouped[c][:].rearrange("p (c i t) -> p c t i", i=4, t=PACK),
                 in0=ys[c][:].rearrange("p t (c i) -> p c t i", i=4),
                 in1=gain2_wide,
                 op=MULT,
             )
-            y_codes, y_scales = quantize(y_grouped[:], "y%d" % c)
+
+        def third_product(c):
+            cols = slice(c * CH, (c + 1) * CH)
+            y_codes, y_scales = quantize(y_grouped[c][:], "y%d" % c)
             acc3 = bank([P, N // P, CH], "acc3_%d" % c, "turn%d" % (c % 2))
             for n in range(N // P):
                 nc.tensor.matmul_mx(
@@ -275,3 +298,13 @@ def tile_list_scanner_recount_features_kernel(
             result = sb([P, N // P, CH], F32, "result%d" % c)
             nc.scalar.copy(out=result[:], in_=acc3[:])
             nc.sync.dma_start(out=out_rows[:, :, cols], in_=result[:])
+
+        for step in range(CHUNKS + 2):
+            for lag, stage in enumerate((read_last, add_ink, second_product)):
+                if 0 <= step - lag < CHUNKS:
+                    stage(step - lag)
+        w3_codes, w3_scales = quantize(w3_grouped[:], "w3")
+        for step in range(CHUNKS + 1):
+            for lag, stage in enumerate((apply_gain2, third_product)):
+                if 0 <= step - lag < CHUNKS:
+                    stage(step - lag)

@@ -44,9 +44,9 @@ def tile_list_scanner_recount_features_kernel(
         def bank(shape, name, tag):
             return psum.tile(shape, F32, name=name, tag=tag)
 
-        def quantize(grouped, name):
+        def quantize(grouped, name, tag=None):
             width = grouped.shape[1] // PACK
-            codes = sb([P, width], U32, name + "_codes")
+            codes = sb([P, width], U32, name + "_codes", tag)
             scales = sb([P, width], U8, name + "_scales")
             nc.vector.quantize_mx(out=codes[:].bitcast(FP8X4), scales=scales[:], in_=grouped)
             return codes, scales
@@ -92,21 +92,18 @@ def tile_list_scanner_recount_features_kernel(
             return grouped
 
         raw0 = [None] * PASSES1
-        tabs = [None] * PASSES1
-        raw0[0] = load_w1(0, 0, 2)
-        raw0[1] = load_w1(0, 1, 2)
+        raw0[0] = load_w1(0, 0, 4)
+        raw0[1] = load_w1(0, 1)
+        raw0[2] = load_w1(0, 2)
         nc.sync.dma_start(pick[:], offs)
         nc.sync.dma_start(put[:], offs2)
-        nc.sync.dma_start(out=gain1_sb[:], in_=gain1.rearrange("(b p t) -> p b t", b=HALVES, t=PACK))
-        tabs[0] = load_tab(0)
         for q in range(4):
             nc.sync.dma_start(
                 out=tab_plane[32 * q : 32 * q + 4 * PASSES1, :].bitcast(I32),
                 in_=tab_scales[:, 4 * q : 4 * q + 4, :].bitcast(I32),
             )
-        raw0[2] = load_w1(0, 2)
-        tabs[1] = load_tab(1)
-        tabs[2] = load_tab(2)
+        tabs = [load_tab(a) for a in range(PASSES1)]
+        nc.sync.dma_start(out=gain1_sb[:], in_=gain1.rearrange("(b p t) -> p b t", b=HALVES, t=PACK))
         wgs_sb = sb([P, S], F32, "wgs_sb")
         nc.sync.dma_start(out=wgs_sb[:], in_=wgs)
 
@@ -114,7 +111,11 @@ def tile_list_scanner_recount_features_kernel(
         picked = []
         picked_plane = sb([P, S], U8, "picked_plane")
         for a in range(PASSES1):
-            w1q[0, a] = quantize(group_w1(raw0[a], 0, a)[:], "w1_0_%d" % a)
+            last = a == PASSES1 - 1
+            if last:
+                nc.vector.tensor_copy(out=picked_plane[:], in_=tab_plane[:].indirect(pick[:]))
+            w1q[0, a] = quantize(group_w1(raw0[a], 0, a)[:], "w1_0_%d" % a, "tab_plane" if last else None)
+        for a in range(PASSES1):
             got = sb([P, S], U32, "picked%d" % a)
             pieces = 2 if a == PASSES1 - 1 else 1
             for s in range(pieces):
@@ -124,8 +125,6 @@ def tile_list_scanner_recount_features_kernel(
                     in_=tabs[a][:].bitcast(U32).indirect(pick[:, s * w // 16 : (s + 1) * w // 16]),
                 )
             picked.append(got)
-            if a == 0:
-                nc.vector.tensor_copy(out=picked_plane[:], in_=tab_plane[:].indirect(pick[:]))
 
         def first_product(b):
             units = [(t, 0, S, "wide%d" % t) for t in range(PACK)]
@@ -231,10 +230,28 @@ def tile_list_scanner_recount_features_kernel(
             in_=w3_raw[:].rearrange("p t (c i) -> p c t i", i=4),
         )
 
-        x1 = sb([P, PACK, S], F32, "x1")
+        x1 = sb([P, PACK, S], F32, "x1", tag="z0_words")
         for t in range(PACK - 1):
             nc.vector.tensor_tensor(out=x1[:, t, :], in0=pages[t][:].indirect(take[:]), in1=wgt_sb[:], op=MULT)
-        acc2 = [bank([P, S], "y_%d" % t, "wide%d" % t) for t in range(PACK)]
+        pair_tags = (("wide0", "wide1"), ("wide2", "wide3"), ("turn0", "turn1"), ("back0", "back1"))
+
+        def second_pass(ps, b, t, codes, scales):
+            nc.tensor.matmul_mx(
+                out=ps[:, t % 2, :],
+                lhsT=w2_codes[:, b, 2 * t * P : 2 * (t + 1) * P].bitcast(FP4X4),
+                lhsT_scale=w2_plane[:, b, t * P : (t + 1) * P],
+                rhs=codes.bitcast(FP8X4),
+                rhs_scale=scales,
+                start=(b == 0 and t % 2 == 0),
+                stop=(b == 1 and t % 2 == 1),
+            )
+
+        acc2 = []
+        for c in range(CHUNKS):
+            cols = slice(c * CH, (c + 1) * CH)
+            acc2.append([bank([P, 2, CH], "y_%d_%d" % (c, u), pair_tags[c][u]) for u in range(2)])
+            for t in range(PACK):
+                second_pass(acc2[c][t // 2], 0, t, z0_codes[:, cols], z0_scales[:, cols])
         gain2_wide = vec[:, PACK : 2 * PACK].unsqueeze(1).unsqueeze(3).to_broadcast([P, CH // 4, PACK, 4])
         out_rows = out.rearrange("(n p) j -> p n j", p=P)
         z1, ys, y_grouped = {}, {}, {}
@@ -256,21 +273,12 @@ def tile_list_scanner_recount_features_kernel(
             )
 
         def second_product(c):
-            cols = slice(c * CH, (c + 1) * CH)
             z1_codes, z1_scales = quantize(z1[c][:], "z1_%d" % c)
             ys[c] = sb([P, PACK, CH], F32, "y_sb%d" % c)
             for t in range(PACK):
-                for b, codes, scales in ((0, z0_codes[:, cols], z0_scales[:, cols]), (1, z1_codes[:], z1_scales[:])):
-                    nc.tensor.matmul_mx(
-                        out=acc2[t][:, cols],
-                        lhsT=w2_codes[:, b, 2 * t * P : 2 * (t + 1) * P].bitcast(FP4X4),
-                        lhsT_scale=w2_plane[:, b, t * P : (t + 1) * P],
-                        rhs=codes.bitcast(FP8X4),
-                        rhs_scale=scales,
-                        start=(b == 0),
-                        stop=(b == 1),
-                    )
-                nc.scalar.activation(out=ys[c][:, t, :], in_=acc2[t][:, cols], func=TANH, bias=vec[:, t : t + 1])
+                second_pass(acc2[c][t // 2], 1, t, z1_codes[:], z1_scales[:])
+            for t in range(PACK):
+                nc.scalar.activation(out=ys[c][:, t, :], in_=acc2[c][t // 2][:, t % 2, :], func=TANH, bias=vec[:, t : t + 1])
 
         def apply_gain2(c):
             y_grouped[c] = sb([P, CH * PACK], BF16, "y_grouped%d" % c)
@@ -284,7 +292,7 @@ def tile_list_scanner_recount_features_kernel(
         def third_product(c):
             cols = slice(c * CH, (c + 1) * CH)
             y_codes, y_scales = quantize(y_grouped[c][:], "y%d" % c)
-            acc3 = bank([P, N // P, CH], "acc3_%d" % c, "turn%d" % (c % 2))
+            acc3 = bank([P, N // P, CH], "acc3_%d" % c, pair_tags[c][0])
             for n in range(N // P):
                 nc.tensor.matmul_mx(
                     out=acc3[:, n, :],

@@ -21,11 +21,16 @@ TANH = mybir.ActivationFunctionType.Tanh
 
 P = 128
 PACK = 4
-KP = P * PACK
-PASSES1 = K // KP
-HALVES = H // KP
-CH = 128
-CHUNKS = S // CH
+K_PASS = P * PACK
+QUADRANTS = 4
+BLOCK_PARTS = 8
+PER_COLUMN = 16
+PASSES1 = K // K_PASS
+HALVES = H // K_PASS
+CHUNK = 128
+CHUNKS = S // CHUNK
+LINE = 4
+FIRST_LOAD_PIECES = 4
 
 
 def tile_list_scanner_recount_features_kernel(
@@ -51,17 +56,24 @@ def tile_list_scanner_recount_features_kernel(
             nc.vector.quantize_mx(out=codes[:].bitcast(FP8X4), scales=scales[:], in_=grouped)
             return codes, scales
 
-        pick = lists.tile([P, S // 16], U16, name="pick")
-        put = lists.tile([P, S // 16], U16, name="put")
-        take = lists.tile([P, S // 16], U16, name="take")
+        def entries(offsets, first, count):
+            return offsets[:, first // PER_COLUMN : (first + count) // PER_COLUMN]
+
+        def as_rows(rows):
+            return rows.rearrange("p t (c i) -> p c t i", i=LINE)
+
+        def as_words(grouped):
+            return grouped.rearrange("p (c i t) -> p c t i", i=LINE, t=PACK)
+
+        pick = lists.tile([P, S // PER_COLUMN], U16, name="pick")
+        put = lists.tile([P, S // PER_COLUMN], U16, name="put")
+        take = lists.tile([P, S // PER_COLUMN], U16, name="take")
 
         tab_plane = sb([P, T], U8, "tab_plane")
         nc.vector.memset(tab_plane[:].bitcast(I32), 0)
         gain1_sb = sb([P, HALVES, PACK], F32, "gain1_sb")
         vec_rows = sb([P, P], F32, "vec_rows")
         nc.vector.memset(vec_rows[:], 0.0)
-        warm = sb([P, 1], F32, "warm")
-        nc.scalar.activation(out=warm[:], in_=vec_rows[:, 0:1], func=TANH)
         pages = [sb([P, T2], F32, "page%d" % t) for t in range(PACK)]
         for t in range(PACK):
             nc.vector.memset(pages[t][:], 0.0)
@@ -71,8 +83,9 @@ def tile_list_scanner_recount_features_kernel(
         make_identity(nc, ident[:])
 
         def load_w1(b, a, pieces=1):
-            raw = sb([P, PACK, KP], F32, "w1_raw_%d_%d" % (b, a), tag="w1_raw%d" % a)
-            rows = w1[a * KP : (a + 1) * KP, b * KP : (b + 1) * KP].rearrange("(p j) c -> p j c", j=PACK)
+            raw = sb([P, PACK, K_PASS], F32, "w1_raw_%d_%d" % (b, a), tag="w1_raw%d" % a)
+            rows = w1[a * K_PASS : (a + 1) * K_PASS, b * K_PASS : (b + 1) * K_PASS]
+            rows = rows.rearrange("(p j) c -> p j c", j=PACK)
             step = PACK // pieces
             for j in range(0, PACK, step):
                 nc.sync.dma_start(out=raw[:, j : j + step, :], in_=rows[:, j : j + step, :])
@@ -84,73 +97,85 @@ def tile_list_scanner_recount_features_kernel(
             return words
 
         def group_w1(raw, b, a):
-            grouped = sb([P, KP * PACK], BF16, "w1_grouped_%d_%d" % (b, a), tag="grouped_%d_%d" % (b, a))
+            grouped = sb([P, K_PASS * PACK], BF16, "w1_grouped_%d_%d" % (b, a), tag="grouped_%d_%d" % (b, a))
             nc.scalar.copy(
                 out=grouped[:].rearrange("p (t m j) -> p m j t", t=PACK, j=PACK),
                 in_=raw[:].rearrange("p j (m t) -> p m j t", t=PACK),
             )
             return grouped
 
-        raw0 = [None] * PASSES1
-        raw0[0] = load_w1(0, 0, 4)
-        raw0[1] = load_w1(0, 1)
-        raw0[2] = load_w1(0, 2)
+        raw0 = [load_w1(0, 0, FIRST_LOAD_PIECES)] + [load_w1(0, a) for a in range(1, PASSES1)]
         nc.sync.dma_start(pick[:], offs)
-        nc.sync.dma_start(put[:], offs2)
-        for q in range(4):
+        nc.sync.dma_start(out=gain1_sb[:], in_=gain1.rearrange("(b p t) -> p b t", b=HALVES, t=PACK))
+        for q in range(QUADRANTS):
             nc.sync.dma_start(
                 out=tab_plane[32 * q : 32 * q + 4 * PASSES1, :].bitcast(I32),
                 in_=tab_scales[:, 4 * q : 4 * q + 4, :].bitcast(I32),
             )
-        tabs = [load_tab(a) for a in range(PASSES1)]
-        nc.sync.dma_start(out=gain1_sb[:], in_=gain1.rearrange("(b p t) -> p b t", b=HALVES, t=PACK))
+        tabs = [load_tab(a) for a in range(PASSES1 - 1)]
+        nc.sync.dma_start(put[:], offs2)
+        tabs.append(load_tab(PASSES1 - 1))
         wgs_sb = sb([P, S], F32, "wgs_sb")
         nc.sync.dma_start(out=wgs_sb[:], in_=wgs)
+        w2_raw = sb([P, HALVES, 2 * M // 4], I32, "w2_raw")
+        nc.sync.dma_start(out=w2_raw[:], in_=w2_words.rearrange("b p c -> p b c").bitcast(I32))
 
         w1q = {}
-        picked = []
         picked_plane = sb([P, S], U8, "picked_plane")
-        for a in range(PASSES1):
-            last = a == PASSES1 - 1
-            if last:
-                nc.vector.tensor_copy(out=picked_plane[:], in_=tab_plane[:].indirect(pick[:]))
-            w1q[0, a] = quantize(group_w1(raw0[a], 0, a)[:], "w1_0_%d" % a, "tab_plane" if last else None)
+        for a in range(PASSES1 - 1):
+            w1q[0, a] = quantize(group_w1(raw0[a], 0, a)[:], "w1_0_%d" % a)
+        nc.vector.tensor_copy(out=picked_plane[:], in_=tab_plane[:].indirect(pick[:]))
+        last_pass = PASSES1 - 1
+        w1q[0, last_pass] = quantize(group_w1(raw0[last_pass], 0, last_pass)[:], "w1_0_last", "tab_plane")
+        picked = []
         for a in range(PASSES1):
             got = sb([P, S], U32, "picked%d" % a)
-            pieces = 2 if a == PASSES1 - 1 else 1
-            for s in range(pieces):
-                w = S // pieces
+            count = S // 2 if a == last_pass else S
+            for first in range(0, S, count):
                 nc.vector.tensor_copy(
-                    out=got[:, s * w : (s + 1) * w],
-                    in_=tabs[a][:].bitcast(U32).indirect(pick[:, s * w // 16 : (s + 1) * w // 16]),
+                    out=got[:, first : first + count],
+                    in_=tabs[a][:].bitcast(U32).indirect(entries(pick, first, count)),
                 )
             picked.append(got)
 
+        w2_codes = sb([P, HALVES, 2 * M], U8, "w2_codes")
+        nc.vector.tensor_copy(
+            out=w2_codes[:].bitcast(I32).rearrange("p b (t a v) -> p b t a v", t=PACK, v=4),
+            in_=w2_raw[:].rearrange("p b (a t v) -> p b t a v", t=PACK, v=4),
+        )
+
         def first_product(b):
-            units = [(t, 0, S, "wide%d" % t) for t in range(PACK)]
+            parts = [(t, 0, S, "wide%d" % t) for t in range(PACK)]
             if b == 0:
-                units = [(0, 0, S // 2, "turn0"), (0, S // 2, S // 2, "wide0")] + units[1:]
-            acc = [bank([P, w], "h_%d_%d_%d" % (b, t, j0), tag) for t, j0, w, tag in units]
-            for a in range(PASSES1):
-                codes, scales = w1q[b, a]
-                for (t, j0, w, tag), ps in zip(units, acc):
-                    cols = slice(t * P, (t + 1) * P)
+                parts = [(0, 0, S // 2, "turn0"), (0, S // 2, S // 2, "wide0")] + parts[1:]
+            sums = [bank([P, count], "h_%d_%d_%d" % (b, t, first), tag) for t, first, count, tag in parts]
+            for (t, first, count, tag), ps in zip(parts, sums):
+                order = [0, 2, 1] if (b == 0 and t > 0) else [0, 1, 2]
+                for a in order:
+                    codes, scales = w1q[b, a]
                     nc.tensor.matmul_mx(
                         out=ps[:],
-                        lhsT=codes[:, cols].bitcast(FP8X4),
-                        lhsT_scale=scales[:, cols],
-                        rhs=picked[a][:, j0 : j0 + w].bitcast(FP8X4),
-                        rhs_scale=picked_plane[4 * a : P, j0 : j0 + w],
-                        start=(a == 0),
-                        stop=(a == PASSES1 - 1),
+                        lhsT=codes[:, t * P : (t + 1) * P].bitcast(FP8X4),
+                        lhsT_scale=scales[:, t * P : (t + 1) * P],
+                        rhs=picked[a][:, first : first + count].bitcast(FP8X4),
+                        rhs_scale=picked_plane[4 * a : P, first : first + count],
+                        start=(a == order[0]),
+                        stop=(a == order[-1]),
                     )
-            for (t, j0, w, tag), ps in zip(units, acc):
-                h = sb([P, w], F32, "h_sb_%d_%d_%d" % (b, t, j0))
+            for (t, first, count, tag), ps in zip(parts, sums):
+                h = sb([P, count], F32, "h_sb_%d_%d_%d" % (b, t, first))
                 nc.scalar.activation(out=h[:], in_=ps[:], func=COPY, scale=gain1_sb[:, b, t : t + 1])
                 nc.vector.tensor_tensor(
-                    out=pages[t][:].indirect(put[:, j0 // 16 : (j0 + w) // 16]),
-                    in0=h[:], in1=wgs_sb[:, j0 : j0 + w], op=MULT,
+                    out=pages[t][:].indirect(entries(put, first, count)),
+                    in0=h[:], in1=wgs_sb[:, first : first + count], op=MULT,
                 )
+
+        def read_page(t, first, count, x):
+            nc.vector.tensor_tensor(
+                out=x[:, t, first : first + count],
+                in0=pages[t][:].indirect(entries(take, first, count)),
+                in1=wgt_sb[:, first : first + count], op=MULT,
+            )
 
         first_product(0)
 
@@ -161,40 +186,36 @@ def tile_list_scanner_recount_features_kernel(
         inks = []
         for b in range(HALVES):
             ink_sb = sb([P, PACK, S], F32, "ink%d" % b)
-            nc.sync.dma_start(out=ink_sb[:], in_=ink[b * KP : (b + 1) * KP, :].rearrange("(p t) j -> p t j", t=PACK))
+            rows = ink[b * K_PASS : (b + 1) * K_PASS, :]
+            nc.sync.dma_start(out=ink_sb[:], in_=rows.rearrange("(p t) j -> p t j", t=PACK))
             inks.append(ink_sb)
-        w2_raw = sb([P, HALVES, 2 * M // 4], I32, "w2_raw")
-        nc.sync.dma_start(out=w2_raw[:], in_=w2_words.rearrange("b p c -> p b c").bitcast(I32))
-        for q in range(4):
+        for q in range(QUADRANTS):
             nc.sync.dma_start(
                 out=w2_plane_raw[32 * q : 32 * q + 4, :, :].bitcast(I32),
                 in_=w2_scales[:, 4 * q : 4 * q + 4, :].rearrange("b r m -> r b m").bitcast(I32),
             )
         w3_raw = sb([P, PACK, N], F32, "w3_raw")
-        w3_dealt = w3.rearrange("(a t e) n -> t a e n", t=PACK, e=8)
+        w3_dealt = w3.rearrange("(a t e) n -> t a e n", t=PACK, e=BLOCK_PARTS)
         for t in range(PACK):
             nc.sync.dma_start(out=w3_raw[:, t, :], in_=w3_dealt[t])
-        nc.sync.dma_start(
-            out=vec_rows[0:PACK, :].rearrange("t (a e) -> t a e", e=8),
-            in_=b2.rearrange("(a t e) -> t a e", t=PACK, e=8),
-        )
-        nc.sync.dma_start(
-            out=vec_rows[PACK : 2 * PACK, :].rearrange("t (a e) -> t a e", e=8),
-            in_=gain2.rearrange("(a t e) -> t a e", t=PACK, e=8),
-        )
+        for first_row, vector in ((0, b2), (PACK, gain2)):
+            nc.sync.dma_start(
+                out=vec_rows[first_row : first_row + PACK, :].rearrange("t (a e) -> t a e", e=BLOCK_PARTS),
+                in_=vector.rearrange("(a t e) -> t a e", t=PACK, e=BLOCK_PARTS),
+            )
 
         for a in range(PASSES1):
             w1q[1, a] = quantize(group_w1(raw1[a], 1, a)[:], "w1_1_%d" % a)
 
-        x0 = sb([P, PACK, S], F32, "x0", tag="grouped_1_2")
+        x0 = sb([P, PACK, S], F32, "x0", tag="grouped_1_%d" % last_pass)
         for t in range(PACK):
-            nc.vector.tensor_tensor(out=x0[:, t, :], in0=pages[t][:].indirect(take[:]), in1=wgt_sb[:], op=MULT)
+            read_page(t, 0, S, x0)
 
         first_product(1)
 
         z0_words = sb([P, S, 2], F32, "z0_words")
         for c in range(CHUNKS):
-            cols = slice(c * CH, (c + 1) * CH)
+            cols = slice(c * CHUNK, (c + 1) * CHUNK)
             summed = bank([P, PACK, P], "summed%d" % c, "turn%d" % (c % 2))
             for t in range(PACK):
                 nc.tensor.matmul(out=summed[:, t, :], lhsT=inks[0][:, t, cols], rhs=ident[:],
@@ -210,11 +231,6 @@ def tile_list_scanner_recount_features_kernel(
             nc.scalar.copy(out=z0_words[:, cols, :], in_=back[:].rearrange("p u j -> p j u"))
         z0_codes, z0_scales = quantize(z0_words[:].rearrange("p j u -> p (j u)").bitcast(BF16), "z0")
 
-        w2_codes = sb([P, HALVES, 2 * M], U8, "w2_codes")
-        nc.vector.tensor_copy(
-            out=w2_codes[:].bitcast(I32).rearrange("p b (t a v) -> p b t a v", t=PACK, v=4),
-            in_=w2_raw[:].rearrange("p b (a t v) -> p b t a v", t=PACK, v=4),
-        )
         w2_plane = sb([P, HALVES, M], U8, "w2_plane")
         nc.vector.tensor_copy(
             out=w2_plane[:].bitcast(I32).rearrange("p b (t a v) -> p b t a v", t=PACK, v=2),
@@ -225,15 +241,13 @@ def tile_list_scanner_recount_features_kernel(
         vec = sb([P, 2 * PACK], F32, "vec")
         nc.scalar.copy(out=vec[:], in_=vec_turned[:, 0 : 2 * PACK])
         w3_grouped = sb([P, N * PACK], BF16, "w3_grouped")
-        nc.scalar.copy(
-            out=w3_grouped[:].rearrange("p (c i t) -> p c t i", i=4, t=PACK),
-            in_=w3_raw[:].rearrange("p t (c i) -> p c t i", i=4),
-        )
+        nc.scalar.copy(out=as_words(w3_grouped[:]), in_=as_rows(w3_raw[:]))
 
         x1 = sb([P, PACK, S], F32, "x1", tag="z0_words")
         for t in range(PACK - 1):
-            nc.vector.tensor_tensor(out=x1[:, t, :], in0=pages[t][:].indirect(take[:]), in1=wgt_sb[:], op=MULT)
-        pair_tags = (("wide0", "wide1"), ("wide2", "wide3"), ("turn0", "turn1"), ("back0", "back1"))
+            read_page(t, 0, S, x1)
+
+        chunk_banks = (("wide0", "wide1"), ("wide2", "wide3"), ("turn0", "turn1"), ("back0", "back1"))
 
         def second_pass(ps, b, t, codes, scales):
             nc.tensor.matmul_mx(
@@ -246,56 +260,46 @@ def tile_list_scanner_recount_features_kernel(
                 stop=(b == 1 and t % 2 == 1),
             )
 
-        acc2 = []
+        sums2 = []
         for c in range(CHUNKS):
-            cols = slice(c * CH, (c + 1) * CH)
-            acc2.append([bank([P, 2, CH], "y_%d_%d" % (c, u), pair_tags[c][u]) for u in range(2)])
+            cols = slice(c * CHUNK, (c + 1) * CHUNK)
+            sums2.append([bank([P, 2, CHUNK], "y_%d_%d" % (c, u), chunk_banks[c][u]) for u in range(2)])
             for t in range(PACK):
-                second_pass(acc2[c][t // 2], 0, t, z0_codes[:, cols], z0_scales[:, cols])
-        gain2_wide = vec[:, PACK : 2 * PACK].unsqueeze(1).unsqueeze(3).to_broadcast([P, CH // 4, PACK, 4])
-        out_rows = out.rearrange("(n p) j -> p n j", p=P)
-        z1, ys, y_grouped = {}, {}, {}
+                second_pass(sums2[c][t // 2], 0, t, z0_codes[:, cols], z0_scales[:, cols])
 
-        def read_last(c):
-            cols = slice(c * CH, (c + 1) * CH)
-            entries = take[:, c * CH // 16 : (c + 1) * CH // 16]
-            t = PACK - 1
-            nc.vector.tensor_tensor(out=x1[:, t, cols], in0=pages[t][:].indirect(entries), in1=wgt_sb[:, cols], op=MULT)
+        gain2_wide = vec[:, PACK : 2 * PACK].unsqueeze(1).unsqueeze(3).to_broadcast([P, CHUNK // LINE, PACK, LINE])
+        z1, tanhs, ys = {}, {}, {}
+
+        def read_last_slice(c):
+            read_page(PACK - 1, c * CHUNK, CHUNK, x1)
 
         def add_ink(c):
-            cols = slice(c * CH, (c + 1) * CH)
-            z1[c] = sb([P, CH * PACK], BF16, "z1_%d" % c)
+            cols = slice(c * CHUNK, (c + 1) * CHUNK)
+            z1[c] = sb([P, CHUNK * PACK], BF16, "z1_%d" % c)
             nc.vector.tensor_tensor(
-                out=z1[c][:].rearrange("p (c i t) -> p c t i", i=4, t=PACK),
-                in0=x1[:, :, cols].rearrange("p t (c i) -> p c t i", i=4),
-                in1=inks[1][:, :, cols].rearrange("p t (c i) -> p c t i", i=4),
-                op=ADD,
+                out=as_words(z1[c][:]), in0=as_rows(x1[:, :, cols]), in1=as_rows(inks[1][:, :, cols]), op=ADD
             )
 
         def second_product(c):
             z1_codes, z1_scales = quantize(z1[c][:], "z1_%d" % c)
-            ys[c] = sb([P, PACK, CH], F32, "y_sb%d" % c)
+            tanhs[c] = sb([P, PACK, CHUNK], F32, "tanh%d" % c)
             for t in range(PACK):
-                second_pass(acc2[c][t // 2], 1, t, z1_codes[:], z1_scales[:])
+                second_pass(sums2[c][t // 2], 1, t, z1_codes[:], z1_scales[:])
             for t in range(PACK):
-                nc.scalar.activation(out=ys[c][:, t, :], in_=acc2[c][t // 2][:, t % 2, :], func=TANH, bias=vec[:, t : t + 1])
+                nc.scalar.activation(
+                    out=tanhs[c][:, t, :], in_=sums2[c][t // 2][:, t % 2, :], func=TANH, bias=vec[:, t : t + 1]
+                )
 
         def apply_gain2(c):
-            y_grouped[c] = sb([P, CH * PACK], BF16, "y_grouped%d" % c)
-            nc.vector.tensor_tensor(
-                out=y_grouped[c][:].rearrange("p (c i t) -> p c t i", i=4, t=PACK),
-                in0=ys[c][:].rearrange("p t (c i) -> p c t i", i=4),
-                in1=gain2_wide,
-                op=MULT,
-            )
+            ys[c] = sb([P, CHUNK * PACK], BF16, "y_grouped%d" % c)
+            nc.vector.tensor_tensor(out=as_words(ys[c][:]), in0=as_rows(tanhs[c][:]), in1=gain2_wide, op=MULT)
 
         def third_product(c):
-            cols = slice(c * CH, (c + 1) * CH)
-            y_codes, y_scales = quantize(y_grouped[c][:], "y%d" % c)
-            acc3 = bank([P, N // P, CH], "acc3_%d" % c, pair_tags[c][0])
+            y_codes, y_scales = quantize(ys[c][:], "y%d" % c)
             for n in range(N // P):
+                ps = bank([P, CHUNK], "out_%d_%d" % (c, n), chunk_banks[c][n])
                 nc.tensor.matmul_mx(
-                    out=acc3[:, n, :],
+                    out=ps[:],
                     lhsT=w3_codes[:, n * P : (n + 1) * P].bitcast(FP8X4),
                     lhsT_scale=w3_scales[:, n * P : (n + 1) * P],
                     rhs=y_codes[:].bitcast(FP8X4),
@@ -303,16 +307,19 @@ def tile_list_scanner_recount_features_kernel(
                     start=True,
                     stop=True,
                 )
-            result = sb([P, N // P, CH], F32, "result%d" % c)
-            nc.scalar.copy(out=result[:], in_=acc3[:])
-            nc.sync.dma_start(out=out_rows[:, :, cols], in_=result[:])
+                result = sb([P, CHUNK], F32, "result%d_%d" % (c, n))
+                if c == CHUNKS - 1 and n == N // P - 1:
+                    nc.vector.tensor_copy(out=result[:], in_=ps[:])
+                else:
+                    nc.scalar.copy(out=result[:], in_=ps[:])
+                nc.sync.dma_start(out=out[n * P : (n + 1) * P, c * CHUNK : (c + 1) * CHUNK], in_=result[:])
 
-        for step in range(CHUNKS + 2):
-            for lag, stage in enumerate((read_last, add_ink, second_product)):
-                if 0 <= step - lag < CHUNKS:
-                    stage(step - lag)
+        def staggered(stages):
+            for step in range(CHUNKS + len(stages) - 1):
+                for lag, stage in enumerate(stages):
+                    if 0 <= step - lag < CHUNKS:
+                        stage(step - lag)
+
+        staggered((read_last_slice, add_ink, second_product))
         w3_codes, w3_scales = quantize(w3_grouped[:], "w3")
-        for step in range(CHUNKS + 1):
-            for lag, stage in enumerate((apply_gain2, third_product)):
-                if 0 <= step - lag < CHUNKS:
-                    stage(step - lag)
+        staggered((apply_gain2, third_product))

from contextlib import ExitStack

import concourse.mybir as mybir
from concourse.masks import make_identity

T, S, T2, K, H, M, N = 2048, 512, 1024, 1536, 1024, 512, 256
FLOPS = 2 * S * (K * H + H * M + M * N)

F32 = mybir.dt.float32
BF16 = mybir.dt.bfloat16
I32 = mybir.dt.int32
U32 = mybir.dt.uint32
U16 = mybir.dt.uint16
U8 = mybir.dt.uint8
FP8X4 = mybir.dt.float8_e4m3fn_x4
FP4X4 = mybir.dt.float4_e2m1fn_x4
MULT = mybir.AluOpType.mult
ADD = mybir.AluOpType.add
COPY = mybir.ActivationFunctionType.Copy
TANH = mybir.ActivationFunctionType.Tanh

P = 128
PACK = 4
K_PASS = P * PACK
QUADRANTS = 4
BLOCK_PARTS = 8
PER_COLUMN = 16
PASSES1 = K // K_PASS
HALVES = H // K_PASS
CHUNK = 128
CHUNKS = S // CHUNK
LINE = 4
FIRST_LOAD_PIECES = 4


def tile_list_scanner_recount_features_kernel(
    tc, tab_words, tab_scales, offs, offs2, offs3, w1, gain1, wgs, wgt, ink,
    w2_words, w2_scales, b2, gain2, w3, out,
):
    nc = tc.nc
    with ExitStack() as ctx:
        lists = ctx.enter_context(tc.tile_pool(name="lists", bufs=1))
        keep = ctx.enter_context(tc.tile_pool(name="keep", bufs=1))
        psum = ctx.enter_context(tc.psum_pool(name="psum", bufs=1))

        def sb(shape, dtype, name, tag=None):
            return keep.tile(shape, dtype, name=name, tag=tag or name, align_bytes=64)

        def bank(shape, name, tag):
            return psum.tile(shape, F32, name=name, tag=tag)

        def quantize(grouped, name, tag=None):
            width = grouped.shape[1] // PACK
            codes = sb([P, width], U32, name + "_codes", tag)
            scales = sb([P, width], U8, name + "_scales")
            nc.vector.quantize_mx(out=codes[:].bitcast(FP8X4), scales=scales[:], in_=grouped)
            return codes, scales

        def entries(offsets, first, count):
            return offsets[:, first // PER_COLUMN : (first + count) // PER_COLUMN]

        def as_rows(rows):
            return rows.rearrange("p t (c i) -> p c t i", i=LINE)

        def as_words(grouped):
            return grouped.rearrange("p (c i t) -> p c t i", i=LINE, t=PACK)

        pick = lists.tile([P, S // PER_COLUMN], U16, name="pick")
        put = lists.tile([P, S // PER_COLUMN], U16, name="put")
        take = lists.tile([P, S // PER_COLUMN], U16, name="take")

        tab_plane = sb([P, T], U8, "tab_plane")
        nc.vector.memset(tab_plane[:].bitcast(I32), 0)
        gain1_sb = sb([P, HALVES, PACK], F32, "gain1_sb")
        vec_rows = sb([P, P], F32, "vec_rows")
        nc.vector.memset(vec_rows[:], 0.0)
        pages = [sb([P, T2], F32, "page%d" % t) for t in range(PACK)]
        for t in range(PACK):
            nc.vector.memset(pages[t][:], 0.0)
        w2_plane_raw = sb([P, HALVES, M], U8, "w2_plane_raw")
        nc.gpsimd.memset(w2_plane_raw[:].rearrange("p b m -> p (b m)").bitcast(I32), 0)
        ident = sb([P, P], F32, "ident")
        make_identity(nc, ident[:])

        def load_w1(b, a, pieces=1):
            raw = sb([P, PACK, K_PASS], F32, "w1_raw_%d_%d" % (b, a), tag="w1_raw%d" % a)
            rows = w1[a * K_PASS : (a + 1) * K_PASS, b * K_PASS : (b + 1) * K_PASS]
            rows = rows.rearrange("(p j) c -> p j c", j=PACK)
            step = PACK // pieces
            for j in range(0, PACK, step):
                nc.sync.dma_start(out=raw[:, j : j + step, :], in_=rows[:, j : j + step, :])
            return raw

        def load_tab(a):
            words = sb([P, T], I32, "tab%d" % a)
            nc.sync.dma_start(out=words[:], in_=tab_words[a].rearrange("p n i -> p (n i)").bitcast(I32))
            return words

        def group_w1(raw, b, a):
            grouped = sb([P, K_PASS * PACK], BF16, "w1_grouped_%d_%d" % (b, a), tag="grouped_%d_%d" % (b, a))
            nc.scalar.copy(
                out=grouped[:].rearrange("p (t m j) -> p m j t", t=PACK, j=PACK),
                in_=raw[:].rearrange("p j (m t) -> p m j t", t=PACK),
            )
            return grouped

        raw0 = [load_w1(0, 0, FIRST_LOAD_PIECES)] + [load_w1(0, a) for a in range(1, PASSES1)]
        nc.sync.dma_start(pick[:], offs)
        nc.sync.dma_start(out=gain1_sb[:], in_=gain1.rearrange("(b p t) -> p b t", b=HALVES, t=PACK))
        for q in range(QUADRANTS):
            nc.sync.dma_start(
                out=tab_plane[32 * q : 32 * q + 4 * PASSES1, :].bitcast(I32),
                in_=tab_scales[:, 4 * q : 4 * q + 4, :].bitcast(I32),
            )
        tabs = [load_tab(a) for a in range(PASSES1 - 1)]
        nc.sync.dma_start(put[:], offs2)
        tabs.append(load_tab(PASSES1 - 1))
        wgs_sb = sb([P, S], F32, "wgs_sb")
        nc.sync.dma_start(out=wgs_sb[:], in_=wgs)
        w2_raw = sb([P, HALVES, 2 * M // 4], I32, "w2_raw")
        nc.sync.dma_start(out=w2_raw[:], in_=w2_words.rearrange("b p c -> p b c").bitcast(I32))

        w1q = {}
        picked_plane = sb([P, S], U8, "picked_plane")
        for a in range(PASSES1 - 1):
            w1q[0, a] = quantize(group_w1(raw0[a], 0, a)[:], "w1_0_%d" % a)
        nc.vector.tensor_copy(out=picked_plane[:], in_=tab_plane[:].indirect(pick[:]))
        last_pass = PASSES1 - 1
        w1q[0, last_pass] = quantize(group_w1(raw0[last_pass], 0, last_pass)[:], "w1_0_last", "tab_plane")
        picked = []
        for a in range(PASSES1):
            got = sb([P, S], U32, "picked%d" % a)
            count = S // 2 if a == last_pass else S
            for first in range(0, S, count):
                nc.vector.tensor_copy(
                    out=got[:, first : first + count],
                    in_=tabs[a][:].bitcast(U32).indirect(entries(pick, first, count)),
                )
            picked.append(got)

        w2_codes = sb([P, HALVES, 2 * M], U8, "w2_codes")
        nc.vector.tensor_copy(
            out=w2_codes[:].bitcast(I32).rearrange("p b (t a v) -> p b t a v", t=PACK, v=4),
            in_=w2_raw[:].rearrange("p b (a t v) -> p b t a v", t=PACK, v=4),
        )

        def first_product(b):
            parts = [(t, 0, S, "wide%d" % t) for t in range(PACK)]
            if b == 0:
                parts = [(0, 0, S // 2, "turn0"), (0, S // 2, S // 2, "wide0")] + parts[1:]
            sums = [bank([P, count], "h_%d_%d_%d" % (b, t, first), tag) for t, first, count, tag in parts]
            for (t, first, count, tag), ps in zip(parts, sums):
                order = [0, 2, 1] if (b == 0 and t > 0) else [0, 1, 2]
                for a in order:
                    codes, scales = w1q[b, a]
                    nc.tensor.matmul_mx(
                        out=ps[:],
                        lhsT=codes[:, t * P : (t + 1) * P].bitcast(FP8X4),
                        lhsT_scale=scales[:, t * P : (t + 1) * P],
                        rhs=picked[a][:, first : first + count].bitcast(FP8X4),
                        rhs_scale=picked_plane[4 * a : P, first : first + count],
                        start=(a == order[0]),
                        stop=(a == order[-1]),
                    )
            for (t, first, count, tag), ps in zip(parts, sums):
                h = sb([P, count], F32, "h_sb_%d_%d_%d" % (b, t, first))
                nc.scalar.activation(out=h[:], in_=ps[:], func=COPY, scale=gain1_sb[:, b, t : t + 1])
                nc.vector.tensor_tensor(
                    out=pages[t][:].indirect(entries(put, first, count)),
                    in0=h[:], in1=wgs_sb[:, first : first + count], op=MULT,
                )

        def read_page(t, first, count, x):
            nc.vector.tensor_tensor(
                out=x[:, t, first : first + count],
                in0=pages[t][:].indirect(entries(take, first, count)),
                in1=wgt_sb[:, first : first + count], op=MULT,
            )

        first_product(0)

        raw1 = [load_w1(1, a) for a in range(PASSES1)]
        nc.sync.dma_start(take[:], offs3)
        wgt_sb = sb([P, S], F32, "wgt_sb")
        nc.sync.dma_start(out=wgt_sb[:], in_=wgt)
        inks = []
        for b in range(HALVES):
            ink_sb = sb([P, PACK, S], F32, "ink%d" % b)
            rows = ink[b * K_PASS : (b + 1) * K_PASS, :]
            nc.sync.dma_start(out=ink_sb[:], in_=rows.rearrange("(p t) j -> p t j", t=PACK))
            inks.append(ink_sb)
        for q in range(QUADRANTS):
            nc.sync.dma_start(
                out=w2_plane_raw[32 * q : 32 * q + 4, :, :].bitcast(I32),
                in_=w2_scales[:, 4 * q : 4 * q + 4, :].rearrange("b r m -> r b m").bitcast(I32),
            )
        w3_raw = sb([P, PACK, N], F32, "w3_raw")
        w3_dealt = w3.rearrange("(a t e) n -> t a e n", t=PACK, e=BLOCK_PARTS)
        for t in range(PACK):
            nc.sync.dma_start(out=w3_raw[:, t, :], in_=w3_dealt[t])
        for first_row, vector in ((0, b2), (PACK, gain2)):
            nc.sync.dma_start(
                out=vec_rows[first_row : first_row + PACK, :].rearrange("t (a e) -> t a e", e=BLOCK_PARTS),
                in_=vector.rearrange("(a t e) -> t a e", t=PACK, e=BLOCK_PARTS),
            )

        for a in range(PASSES1):
            w1q[1, a] = quantize(group_w1(raw1[a], 1, a)[:], "w1_1_%d" % a)

        x0 = sb([P, PACK, S], F32, "x0", tag="grouped_1_%d" % last_pass)
        for t in range(PACK):
            read_page(t, 0, S, x0)

        first_product(1)

        z0_words = sb([P, S, 2], F32, "z0_words")
        for c in range(CHUNKS):
            cols = slice(c * CHUNK, (c + 1) * CHUNK)
            summed = bank([P, PACK, P], "summed%d" % c, "turn%d" % (c % 2))
            for t in range(PACK):
                nc.tensor.matmul(out=summed[:, t, :], lhsT=inks[0][:, t, cols], rhs=ident[:],
                                 is_transpose=True, start=True, stop=False)
                nc.tensor.matmul(out=summed[:, t, :], lhsT=x0[:, t, cols], rhs=ident[:],
                                 is_transpose=True, start=False, stop=True)
            turned = sb([P, 2, P, 2], BF16, "turned%d" % c, tag="turned%d" % (c % 2))
            nc.scalar.copy(out=turned[:], in_=summed[:].rearrange("j (u e) p -> j u p e", e=2))
            turned_words = turned[:].rearrange("j u p e -> j (u p e)").bitcast(F32)
            back = bank([P, 2, P], "back%d" % c, "back%d" % (c % 2))
            for u in range(2):
                nc.tensor.transpose(back[:, u, :], turned_words[:, u * P : (u + 1) * P], ident[:])
            nc.scalar.copy(out=z0_words[:, cols, :], in_=back[:].rearrange("p u j -> p j u"))
        z0_codes, z0_scales = quantize(z0_words[:].rearrange("p j u -> p (j u)").bitcast(BF16), "z0")

        w2_plane = sb([P, HALVES, M], U8, "w2_plane")
        nc.vector.tensor_copy(
            out=w2_plane[:].bitcast(I32).rearrange("p b (t a v) -> p b t a v", t=PACK, v=2),
            in_=w2_plane_raw[:].bitcast(I32).rearrange("p b (a t v) -> p b t a v", t=PACK, v=2),
        )
        vec_turned = bank([P, P], "vec_turned", "back0")
        nc.tensor.transpose(vec_turned[:], vec_rows[:], ident[:])
        vec = sb([P, 2 * PACK], F32, "vec")
        nc.scalar.copy(out=vec[:], in_=vec_turned[:, 0 : 2 * PACK])
        w3_grouped = sb([P, N * PACK], BF16, "w3_grouped")
        nc.scalar.copy(out=as_words(w3_grouped[:]), in_=as_rows(w3_raw[:]))

        x1 = sb([P, PACK, S], F32, "x1", tag="z0_words")
        for t in range(PACK - 1):
            read_page(t, 0, S, x1)

        chunk_banks = (("wide0", "wide1"), ("wide2", "wide3"), ("turn0", "turn1"), ("back0", "back1"))

        def second_pass(ps, b, t, codes, scales):
            nc.tensor.matmul_mx(
                out=ps[:, t % 2, :],
                lhsT=w2_codes[:, b, 2 * t * P : 2 * (t + 1) * P].bitcast(FP4X4),
                lhsT_scale=w2_plane[:, b, t * P : (t + 1) * P],
                rhs=codes.bitcast(FP8X4),
                rhs_scale=scales,
                start=(b == 0 and t % 2 == 0),
                stop=(b == 1 and t % 2 == 1),
            )

        sums2 = []
        for c in range(CHUNKS):
            cols = slice(c * CHUNK, (c + 1) * CHUNK)
            sums2.append([bank([P, 2, CHUNK], "y_%d_%d" % (c, u), chunk_banks[c][u]) for u in range(2)])
            for t in range(PACK):
                second_pass(sums2[c][t // 2], 0, t, z0_codes[:, cols], z0_scales[:, cols])

        gain2_wide = vec[:, PACK : 2 * PACK].unsqueeze(1).unsqueeze(3).to_broadcast([P, CHUNK // LINE, PACK, LINE])
        z1, tanhs, ys = {}, {}, {}

        def read_last_slice(c):
            read_page(PACK - 1, c * CHUNK, CHUNK, x1)

        def add_ink(c):
            cols = slice(c * CHUNK, (c + 1) * CHUNK)
            z1[c] = sb([P, CHUNK * PACK], BF16, "z1_%d" % c)
            nc.vector.tensor_tensor(
                out=as_words(z1[c][:]), in0=as_rows(x1[:, :, cols]), in1=as_rows(inks[1][:, :, cols]), op=ADD
            )

        def second_product(c):
            z1_codes, z1_scales = quantize(z1[c][:], "z1_%d" % c)
            tanhs[c] = sb([P, PACK, CHUNK], F32, "tanh%d" % c)
            for t in range(PACK):
                second_pass(sums2[c][t // 2], 1, t, z1_codes[:], z1_scales[:])
            for t in range(PACK):
                nc.scalar.activation(
                    out=tanhs[c][:, t, :], in_=sums2[c][t // 2][:, t % 2, :], func=TANH, bias=vec[:, t : t + 1]
                )

        def apply_gain2(c):
            ys[c] = sb([P, CHUNK * PACK], BF16, "y_grouped%d" % c)
            nc.vector.tensor_tensor(out=as_words(ys[c][:]), in0=as_rows(tanhs[c][:]), in1=gain2_wide, op=MULT)

        def third_product(c):
            y_codes, y_scales = quantize(ys[c][:], "y%d" % c)
            for n in range(N // P):
                ps = bank([P, CHUNK], "out_%d_%d" % (c, n), chunk_banks[c][n])
                nc.tensor.matmul_mx(
                    out=ps[:],
                    lhsT=w3_codes[:, n * P : (n + 1) * P].bitcast(FP8X4),
                    lhsT_scale=w3_scales[:, n * P : (n + 1) * P],
                    rhs=y_codes[:].bitcast(FP8X4),
                    rhs_scale=y_scales[:],
                    start=True,
                    stop=True,
                )
                result = sb([P, CHUNK], F32, "result%d_%d" % (c, n))
                if c == CHUNKS - 1 and n == N // P - 1:
                    nc.vector.tensor_copy(out=result[:], in_=ps[:])
                else:
                    nc.scalar.copy(out=result[:], in_=ps[:])
                nc.sync.dma_start(out=out[n * P : (n + 1) * P, c * CHUNK : (c + 1) * CHUNK], in_=result[:])

        def staggered(stages):
            for step in range(CHUNKS + len(stages) - 1):
                for lag, stage in enumerate(stages):
                    if 0 <= step - lag < CHUNKS:
                        stage(step - lag)

        staggered((read_last_slice, add_ink, second_product))
        w3_codes, w3_scales = quantize(w3_grouped[:], "w3")
        staggered((apply_gain2, third_product))
